import numpy as np
import ml_dtypes


def mxq(x, axis, fmt="e4m3"):
    dtype, down = {"e4m3": (ml_dtypes.float8_e4m3fn, 7), "e5m2": (ml_dtypes.float8_e5m2, 14)}[fmt]
    v = np.moveaxis(np.asarray(x, np.float32).astype(ml_dtypes.bfloat16).astype(np.float64), axis, -1)
    blocks = v.reshape(v.shape[:-1] + (-1, 32))
    amax = np.abs(blocks).max(-1, keepdims=True)
    byte = np.maximum(np.where(amax > 0, np.frexp(amax)[1] - 1 + 127, 0) - down, 1)
    scale = np.exp2(byte - 127.0)
    codes = (blocks / scale).astype(np.float32).astype(dtype).astype(np.float64)
    return np.moveaxis((codes * scale).reshape(v.shape), -1, axis)


WIDE = False


def mx_kscale(k):
    if not WIDE:
        return np.ones(k)
    levels = np.array([30, -30])
    if k % 512:
        return np.exp2(np.random.permutation(np.resize(levels, k // 32))).repeat(32)
    a = np.empty((k // 512, 16))
    for p in range(k // 512):
        a[p, :8] = np.random.permutation(np.resize(levels, 8))
        for g in range(8):
            far = levels[np.abs(levels - a[p, g]) >= 10]
            a[p, g + 8] = far[np.random.randint(len(far))]
    return np.exp2(a.ravel()).repeat(32)


def f64(x):
    return np.asarray(x).astype(np.float64)


def striped(idx):
    return np.tile(np.asarray(idx).reshape(-1, 16).T, (8, 1)).astype(np.uint16)


def unstriped(offs):
    return offs[:16].T.reshape(-1).astype(np.int64)


E2M1 = np.array([0.0, 0.5, 1.0, 1.5, 2.0, 3.0, 4.0, 6.0, -0.0, -0.5, -1.0, -1.5, -2.0, -3.0, -4.0, -6.0])


def pack_weight(w, fmt):
    k, n = w.shape
    w = f64(np.asarray(w, np.float32).astype(ml_dtypes.bfloat16)).reshape(k // 32, 32, n)
    amax = np.abs(w).max(1)
    if fmt in ("e4m3", "e5m2"):
        byte = np.frexp(amax)[1] - 1 + 127 - (7 if fmt == "e4m3" else 14)
    else:
        mant, ex = np.frexp(amax / 6.0)
        byte = np.where(mant > 0.5, ex, ex - 1) + 127
    byte = np.clip(np.where(amax > 0, byte, 1), 1, 254)
    scaled = (w * np.exp2(127.0 - byte)[:, None, :]).reshape(k, n).astype(np.float32)
    by_word = np.ascontiguousarray(scaled.reshape(k // 512, 128, 4, n).transpose(0, 1, 3, 2))
    if fmt in ("e4m3", "e5m2"):
        words = by_word.astype(ml_dtypes.float8_e4m3fn if fmt == "e4m3" else ml_dtypes.float8_e5m2).view(np.uint8)
    else:
        c = by_word.astype(ml_dtypes.float4_e2m1fn).view(np.uint8) & 0xF
        words = (c[..., 0::2] | (c[..., 1::2] << 4)).reshape(k // 512, 128, 2 * n)
    return np.ascontiguousarray(words), np.ascontiguousarray(byte.astype(np.uint8).reshape(k // 512, 16, n))


def unpack_weight(words, scales, fmt):
    g, _, n = scales.shape
    words = np.ascontiguousarray(words).reshape(g, 128, n, -1)
    if fmt in ("e4m3", "e5m2"):
        vals = words.view(ml_dtypes.float8_e4m3fn if fmt == "e4m3" else ml_dtypes.float8_e5m2).astype(np.float64)
    else:
        nib = np.empty((g, 128, n, 4), np.uint8)
        nib[..., 0::2] = words & 0xF
        nib[..., 1::2] = words >> 4
        vals = E2M1[nib]
    vals = vals * np.repeat(np.exp2(scales.astype(np.float64) - 127.0), 8, axis=1)[..., None]
    return vals.transpose(0, 1, 3, 2).reshape(g * 512, n)


def bf(x):
    return np.asarray(x, np.float32).astype(ml_dtypes.bfloat16)


def planes(Y):
    r, m = Y.shape
    b = f64(bf(Y)).reshape(r // 32, 32, m)
    amax = np.abs(b).max(1)
    byte = np.clip(np.where(amax > 0, np.frexp(amax)[1] - 1 + 127 - 7, 1), 1, 254)
    codes = (b * np.exp2(127.0 - byte)[:, None, :]).reshape(r, m).astype(np.float32).astype(ml_dtypes.float8_e4m3fn).view(np.uint8)
    words = codes.reshape(r // 512, 128, 4, m).transpose(0, 1, 3, 2)
    return np.ascontiguousarray(words), np.ascontiguousarray(byte.astype(np.uint8).reshape(r // 512, 16, m))


K, T, Z, J, R, N, L, E = 512, 1024, 1024, 256, 512, 512, 512, 1024


def setup_inputs():
    n = np.random.standard_normal
    idx = np.random.permutation(T)[:J]
    idx2 = np.random.permutation(Z)[:J]
    idx3 = np.random.permutation(E)[:J]
    fk = mx_kscale(K)
    fr = mx_kscale(R)
    fl = mx_kscale(L)
    xtp = pack_weight(n((K, T)) / fk[:, None], "e4m3")
    xop = pack_weight(n((K, Z)) / fk[:, None], "e2m1")
    wp = pack_weight(n((K, R)) * 1 / np.sqrt(K) * fk[:, None] * fr, "e5m2")
    w2p = pack_weight(n((K, R)) * 1 / np.sqrt(K) * fk[:, None] * fr, "e5m2")
    wbp = pack_weight(n((R, N)) * 1 / np.sqrt(R) / fr[:, None], "e5m2")
    sxp = pack_weight(n((L, J)) / fl[:, None], "e2m1")
    wsp = pack_weight(n((L, N)) * 1 / np.sqrt(L) * fl[:, None], "e5m2")
    return {
        "xt_words": xtp[0],
        "xt_scales": xtp[1],
        "xo_words": xop[0],
        "xo_scales": xop[1],
        "w_words": wp[0],
        "w_scales": wp[1],
        "w2_words": w2p[0],
        "w2_scales": w2p[1],
        "wb_words": wbp[0],
        "wb_scales": wbp[1],
        "sx_words": sxp[0],
        "sx_scales": sxp[1],
        "ws_words": wsp[0],
        "ws_scales": wsp[1],
        "tz": (n((N, E))).astype(np.float32),
        "offs": striped(idx),
        "offs2": striped(idx2),
        "offs3": striped(idx3),
    }


def reference(xt_words, xt_scales, xo_words, xo_scales, w_words, w_scales, w2_words, w2_scales, wb_words, wb_scales, sx_words, sx_scales, ws_words, ws_scales, tz, offs, offs2, offs3):
    idx = unstriped(offs)
    idx2 = unstriped(offs2)
    idx3 = unstriped(offs3)
    xtu = unpack_weight(xt_words, xt_scales, "e4m3")
    xou = unpack_weight(xo_words, xo_scales, "e2m1")
    wu = unpack_weight(w_words, w_scales, "e5m2")
    w2u = unpack_weight(w2_words, w2_scales, "e5m2")
    wbu = unpack_weight(wb_words, wb_scales, "e5m2")
    sxu = unpack_weight(sx_words, sx_scales, "e2m1")
    wsu = unpack_weight(ws_words, ws_scales, "e5m2")
    xtidxg = xtu[:, idx]
    xoidx2g = xou[:, idx2]
    a = wu.T @ xtidxg + w2u.T @ xoidx2g
    b = w2u.T @ xtidxg + wu.T @ xoidx2g
    hid = np.maximum(a, b)
    hidq = mxq(hid, 0, "e4m3")
    p = wbu.T @ hidq + wsu.T @ sxu
    y = p + f64(tz)[:, idx3]
    words, scales = planes(y)
    return y, words, scales

@@ -1,0 +1,166 @@
+from contextlib import ExitStack
+
+import concourse.mybir as mybir
+
+K, T, Z, J, R, N, L, E = 512, 1024, 1024, 256, 512, 512, 512, 1024
+FLOPS = 2 * 512 * 512 * 256 * 6
+
+F32 = mybir.dt.float32
+BF16 = mybir.dt.bfloat16
+I32 = mybir.dt.int32
+U32 = mybir.dt.uint32
+U16 = mybir.dt.uint16
+U8 = mybir.dt.uint8
+E4M3 = mybir.dt.float8_e4m3fn_x4
+E5M2 = mybir.dt.float8_e5m2_x4
+E2M1 = mybir.dt.float4_e2m1fn_x4
+ACT = mybir.ActivationFunctionType
+ALU = mybir.AluOpType
+
+P = 128
+PACK = 4
+HALF = J // 2
+ROWS = 16
+
+XT0, XO0, W0 = 0, J, 2 * J
+SX0 = W0 + 4 * R
+SCALE_COLS = SX0 + J
+
+
+def words8(ap):
+    return ap[0].rearrange("p c r -> p (c r)").bitcast(I32)
+
+
+def tile_list_crossed_direct_skip_tabled_pl_kernel(
+    tc, xt_words, xt_scales, xo_words, xo_scales, w_words, w_scales, w2_words, w2_scales,
+    wb_words, wb_scales, sx_words, sx_scales, ws_words, ws_scales, tz, offs, offs2, offs3,
+    out_0, out_1, out_2,
+):
+    nc = tc.nc
+    with ExitStack() as ctx:
+        lists = ctx.enter_context(tc.tile_pool(name="lists", bufs=1))
+        sb = ctx.enter_context(tc.tile_pool(name="sb", bufs=1))
+        psum = ctx.enter_context(tc.psum_pool(name="psum", bufs=1))
+
+        l_xt = lists.tile([P, J // 16], U16)
+        l_xo = lists.tile([P, J // 16], U16)
+        l_tz = lists.tile([P, J // 16], U16)
+
+        xt_sc = sb.tile([P, T], U8, align_bytes=64)
+        xo_sc = sb.tile([P, Z], U8, align_bytes=64)
+        scales = sb.tile([P, SCALE_COLS], U8, align_bytes=64)
+        nc.vector.memset(xt_sc[:].bitcast(I32), 0)
+        nc.vector.memset(xo_sc[:].bitcast(I32), 0)
+        nc.vector.memset(scales[:, W0 : W0 + 2 * R].bitcast(I32), 0)
+        nc.gpsimd.memset(scales[:, W0 + 2 * R :].bitcast(I32), 0)
+
+        xt_w = sb.tile([P, T], U32, align_bytes=64, tag="xt_then_ws")
+        xo_w = sb.tile([P, Z], U16, align_bytes=64)
+        w_raw = sb.tile([P, R], U32, align_bytes=64, tag="w_then_tz")
+        w2_raw = sb.tile([P, R], U32, align_bytes=64)
+
+        wb_raw = sb.tile([P, N], U32, align_bytes=64)
+        nc.sync.dma_start(l_xt[:], offs)
+        nc.sync.dma_start(xt_sc[0:ROWS, :].bitcast(I32), xt_scales[0].bitcast(I32))
+        nc.sync.dma_start(l_xo[:], offs2)
+        nc.sync.dma_start(xo_sc[0:ROWS, :].bitcast(I32), xo_scales[0].bitcast(I32))
+        nc.sync.dma_start(xt_w[:].bitcast(I32), words8(xt_words))
+        nc.sync.dma_start(xo_w[:].bitcast(I32), xo_words[0].bitcast(I32))
+        for i, sc in enumerate((w_scales, w2_scales, wb_scales, ws_scales)):
+            nc.sync.dma_start(scales[0:ROWS, W0 + i * R : W0 + (i + 1) * R].bitcast(I32), sc[0].bitcast(I32))
+        nc.sync.dma_start(scales[0:ROWS, SX0 : SX0 + J].bitcast(I32), sx_scales[0].bitcast(I32))
+        nc.sync.dma_start(w_raw[:].bitcast(I32), words8(w_words))
+        nc.sync.dma_start(w2_raw[:].bitcast(I32), words8(w2_words))
+        nc.sync.dma_start(l_tz[:], offs3)
+        nc.sync.dma_start(wb_raw[:].bitcast(I32), words8(wb_words))
+
+        xt_sc_g = sb.tile([P, J], U8, align_bytes=64)
+        xo_sc_g = sb.tile([P, J], U8, align_bytes=64)
+        nc.vector.tensor_copy(xt_sc_g[:], xt_sc[:].indirect(l_xt[:]))
+        nc.vector.tensor_copy(xo_sc_g[:], xo_sc[:].indirect(l_xo[:]))
+        nc.vector.tensor_copy(scales[:, XT0 : XT0 + J].bitcast(I32), xt_sc_g[:].bitcast(I32))
+        nc.vector.tensor_copy(scales[:, XO0 : XO0 + J].bitcast(I32), xo_sc_g[:].bitcast(I32))
+        for q in range(1, 4):
+            nc.sync.dma_start(scales[32 * q : 32 * q + 4, :].bitcast(I32), scales[4 * q : 4 * q + 4, :].bitcast(I32))
+
+        xt_g = sb.tile([P, J], U32, align_bytes=64)
+        xo_g = sb.tile([P, J], U16, align_bytes=64)
+        nc.vector.tensor_copy(xt_g[:], xt_w[:].indirect(l_xt[:]))
+        nc.vector.tensor_copy(xo_g[:], xo_w[:].indirect(l_xo[:]))
+
+        late_w = sb.tile([P, N + J // 2], U32, align_bytes=64, tag="xt_then_ws")
+        nc.sync.dma_start(late_w[:, 0:N].bitcast(I32), words8(ws_words))
+        nc.sync.dma_start(late_w[:, N:].bitcast(I32), sx_words[0].bitcast(I32))
+
+        def deal(copy, dealt, raw):
+            copy(dealt.rearrange("p (t m) -> p m t", t=PACK), raw.rearrange("p (m t) -> p m t", t=PACK))
+
+        dealt_w = [sb.tile([P, R], U32, align_bytes=64, name="dealt_w%d" % i) for i in range(4)]
+        dealt_sc = [sb.tile([P, R], U8, align_bytes=64, name="dealt_sc%d" % i) for i in range(4)]
+        deal(nc.vector.tensor_copy, dealt_w[0][:], w_raw[:])
+        tz_sb = sb.tile([P, PACK, E], F32, align_bytes=64, tag="w_then_tz")
+        tz_rows = tz.rearrange("(p t) e -> p t e", t=PACK)
+        for t in range(PACK):
+            nc.sync.dma_start(tz_sb[:, t, :], tz_rows[:, t, :])
+        deal(nc.vector.tensor_copy, dealt_w[1][:], w2_raw[:])
+        for i in range(4):
+            deal(nc.vector.tensor_copy, dealt_sc[i][:], scales[:, W0 + i * R : W0 + (i + 1) * R])
+        deal(nc.vector.tensor_copy, dealt_w[2][:], wb_raw[:])
+        deal(nc.vector.tensor_copy, dealt_w[3][:], late_w[:, 0:N])
+
+        def passes(bank, i, moving, moving_sc, start, stop):
+            for t in range(PACK):
+                cols = slice(t * P, (t + 1) * P)
+                nc.tensor.matmul_mx(
+                    bank[:, t, :], lhsT=dealt_w[i][:, cols].bitcast(E5M2), lhsT_scale=dealt_sc[i][:, cols],
+                    rhs=moving, rhs_scale=moving_sc, start=(start and t == 0), stop=(stop and t == PACK - 1),
+                )
+
+        hid_w = sb.tile([P, J], U32, align_bytes=64)
+        hid_sc = [sb.tile([P, HALF], U8, align_bytes=64, name="hid_sc%d" % h) for h in range(2)]
+        for h in range(2):
+            js = slice(h * HALF, (h + 1) * HALF)
+            xt_h = xt_g[:, js].bitcast(E4M3)
+            xo_h = xo_g[:, js].bitcast(E2M1)
+            xt_s = scales[:, XT0 + h * HALF : XT0 + (h + 1) * HALF]
+            xo_s = scales[:, XO0 + h * HALF : XO0 + (h + 1) * HALF]
+            a = psum.tile([P, PACK, HALF], F32, name="a%d" % h)
+            b = psum.tile([P, PACK, HALF], F32, name="b%d" % h)
+            passes(a, 0, xt_h, xt_s, True, False)
+            passes(a, 1, xo_h, xo_s, False, True)
+            passes(b, 1, xt_h, xt_s, True, False)
+            passes(b, 0, xo_h, xo_s, False, True)
+            a_sb = sb.tile([P, HALF, PACK], F32, name="a_sb%d" % h)
+            nc.scalar.activation(a_sb[:], a[:].rearrange("p t j -> p j t"), ACT.Copy)
+            hid = sb.tile([P, HALF, PACK], BF16, align_bytes=64, name="hid%d" % h)
+            nc.vector.tensor_tensor(hid[:], b[:].rearrange("p t j -> p j t"), a_sb[:], ALU.max)
+            nc.vector.quantize_mx(hid_w[:, js].bitcast(E4M3), hid_sc[h][:], hid[:].rearrange("p j t -> p (j t)"))
+
+        tz_g = sb.tile([P, PACK, J], F32)
+        for t in range(PACK):
+            nc.scalar.activation(tz_g[:, t, :], tz_sb[:, t, :].indirect(l_tz[:]), ACT.Copy)
+
+        y_w = sb.tile([P, J], U32, align_bytes=64)
+        y_sc = sb.tile([P, J], U8, align_bytes=64)
+        out_rows = out_0.rearrange("(p t) j -> p t j", t=PACK)
+        out_words = words8(out_1)
+        sx_w = late_w[:, N:].bitcast(U16)
+        for h in range(2):
+            js = slice(h * HALF, (h + 1) * HALF)
+            acc = psum.tile([P, PACK, HALF], F32, name="acc%d" % h)
+            passes(acc, 3, sx_w[:, js].bitcast(E2M1), scales[:, SX0 + h * HALF : SX0 + (h + 1) * HALF], True, False)
+            passes(acc, 2, hid_w[:, js].bitcast(E4M3), hid_sc[h][:], False, True)
+            y = sb.tile([P, PACK, HALF], F32, name="y%d" % h)
+            nc.vector.tensor_tensor(y[:], acc[:], tz_g[:, :, js], ALU.add)
+            nc.sync.dma_start(out_rows[:, :, js], y[:])
+            y_bf = sb.tile([P, HALF, PACK], BF16, align_bytes=64, name="y_bf%d" % h)
+            if h == 0:
+                nc.scalar.copy(y_bf[:], y[:].rearrange("p t j -> p j t"))
+            else:
+                nc.vector.tensor_copy(y_bf[:], y[:].rearrange("p t j -> p j t"))
+            nc.vector.quantize_mx(y_w[:, js].bitcast(E4M3), y_sc[:, js], y_bf[:].rearrange("p j t -> p (j t)"))
+            nc.sync.dma_start(out_words[:, js], y_w[:, js].bitcast(I32))
+        out_sc = out_2[0].bitcast(I32)
+        for q in range(4):
+            eng = nc.scalar if q % 2 else nc.sync
+            eng.dma_start(out_sc[4 * q : 4 * q + 4, :], y_sc[32 * q : 32 * q + 4, :].bitcast(I32))

@@ -40,6 +40,7 @@ def tile_list_crossed_direct_skip_tabled_pl_kernel(
     with ExitStack() as ctx:
         lists = ctx.enter_context(tc.tile_pool(name="lists", bufs=1))
         sb = ctx.enter_context(tc.tile_pool(name="sb", bufs=1))
+        shared = ctx.enter_context(tc.tile_pool(name="shared", bufs=1))
         psum = ctx.enter_context(tc.psum_pool(name="psum", bufs=1))
 
         l_xt = lists.tile([P, J // 16], U16)
@@ -49,26 +50,28 @@ def tile_list_crossed_direct_skip_tabled_pl_kernel(
         xt_sc = sb.tile([P, T], U8, align_bytes=64)
         xo_sc = sb.tile([P, Z], U8, align_bytes=64)
         scales = sb.tile([P, SCALE_COLS], U8, align_bytes=64)
+        staged = sb.tile([ROWS, SCALE_COLS], U8, align_bytes=64)
+        sx_sc = shared.tile([ROWS, J], U8, align_bytes=64, offset=2432)
         nc.vector.memset(xt_sc[:].bitcast(I32), 0)
         nc.vector.memset(xo_sc[:].bitcast(I32), 0)
-        nc.vector.memset(scales[:, W0 : W0 + 2 * R].bitcast(I32), 0)
-        nc.gpsimd.memset(scales[:, W0 + 2 * R :].bitcast(I32), 0)
+        nc.vector.memset(scales[:].bitcast(I32), 0)
 
-        xt_w = sb.tile([P, T], U32, align_bytes=64, tag="xt_then_ws")
+        xt_w = sb.tile([P, T], U32, align_bytes=64)
         xo_w = sb.tile([P, Z], U16, align_bytes=64)
-        w_raw = sb.tile([P, R], U32, align_bytes=64, tag="w_then_tz")
+        w_raw = sb.tile([P, R], U32, align_bytes=64)
         w2_raw = sb.tile([P, R], U32, align_bytes=64)
-
         wb_raw = sb.tile([P, N], U32, align_bytes=64)
+
+        small = nc.sync
         nc.sync.dma_start(l_xt[:], offs)
-        nc.sync.dma_start(xt_sc[0:ROWS, :].bitcast(I32), xt_scales[0].bitcast(I32))
         nc.sync.dma_start(l_xo[:], offs2)
-        nc.sync.dma_start(xo_sc[0:ROWS, :].bitcast(I32), xo_scales[0].bitcast(I32))
+        small.dma_start(xt_sc[0:ROWS, :].bitcast(I32), xt_scales[0].bitcast(I32))
+        small.dma_start(xo_sc[0:ROWS, :].bitcast(I32), xo_scales[0].bitcast(I32))
         nc.sync.dma_start(xt_w[:].bitcast(I32), words8(xt_words))
         nc.sync.dma_start(xo_w[:].bitcast(I32), xo_words[0].bitcast(I32))
         for i, sc in enumerate((w_scales, w2_scales, wb_scales, ws_scales)):
-            nc.sync.dma_start(scales[0:ROWS, W0 + i * R : W0 + (i + 1) * R].bitcast(I32), sc[0].bitcast(I32))
-        nc.sync.dma_start(scales[0:ROWS, SX0 : SX0 + J].bitcast(I32), sx_scales[0].bitcast(I32))
+            small.dma_start(staged[:, W0 + i * R : W0 + (i + 1) * R].bitcast(I32), sc[0].bitcast(I32))
+        small.dma_start(sx_sc[:].bitcast(I32), sx_scales[0].bitcast(I32))
         nc.sync.dma_start(w_raw[:].bitcast(I32), words8(w_words))
         nc.sync.dma_start(w2_raw[:].bitcast(I32), words8(w2_words))
         nc.sync.dma_start(l_tz[:], offs3)
@@ -78,35 +81,42 @@ def tile_list_crossed_direct_skip_tabled_pl_kernel(
         xo_sc_g = sb.tile([P, J], U8, align_bytes=64)
         nc.vector.tensor_copy(xt_sc_g[:], xt_sc[:].indirect(l_xt[:]))
         nc.vector.tensor_copy(xo_sc_g[:], xo_sc[:].indirect(l_xo[:]))
-        nc.vector.tensor_copy(scales[:, XT0 : XT0 + J].bitcast(I32), xt_sc_g[:].bitcast(I32))
-        nc.vector.tensor_copy(scales[:, XO0 : XO0 + J].bitcast(I32), xo_sc_g[:].bitcast(I32))
-        for q in range(1, 4):
-            nc.sync.dma_start(scales[32 * q : 32 * q + 4, :].bitcast(I32), scales[4 * q : 4 * q + 4, :].bitcast(I32))
+        nc.vector.tensor_copy(staged[:, XT0 : XT0 + J].bitcast(I32), xt_sc_g[0:ROWS, :].bitcast(I32))
+        nc.vector.tensor_copy(staged[:, XO0 : XO0 + J].bitcast(I32), xo_sc_g[0:ROWS, :].bitcast(I32))
+        nc.scalar.copy(staged[:, SX0:].bitcast(U32), sx_sc[:].bitcast(U32))
+        for q in range(4):
+            nc.sync.dma_start(scales[32 * q : 32 * q + 4, :].bitcast(I32), staged[4 * q : 4 * q + 4, :].bitcast(I32))
+
+        late_w = shared.tile([P, N + J // 2], U32, align_bytes=64, offset=0)
+        tz_sb = shared.tile([P, PACK, E], F32, align_bytes=64, offset=2560)
+        nc.sync.dma_start(late_w[:, 0:N].bitcast(I32), words8(ws_words))
+        nc.sync.dma_start(late_w[:, N:].bitcast(I32), sx_words[0].bitcast(I32))
+        tz_rows = tz.rearrange("(p t) e -> p t e", t=PACK)
+        for t in range(PACK):
+            nc.sync.dma_start(tz_sb[:, t, :], tz_rows[:, t, :])
 
         xt_g = sb.tile([P, J], U32, align_bytes=64)
         xo_g = sb.tile([P, J], U16, align_bytes=64)
         nc.vector.tensor_copy(xt_g[:], xt_w[:].indirect(l_xt[:]))
         nc.vector.tensor_copy(xo_g[:], xo_w[:].indirect(l_xo[:]))
 
-        late_w = sb.tile([P, N + J // 2], U32, align_bytes=64, tag="xt_then_ws")
-        nc.sync.dma_start(late_w[:, 0:N].bitcast(I32), words8(ws_words))
-        nc.sync.dma_start(late_w[:, N:].bitcast(I32), sx_words[0].bitcast(I32))
+        def deal(dealt, raw):
+            nc.vector.tensor_copy(dealt.rearrange("p (t m) -> p m t", t=PACK), raw.rearrange("p (m t) -> p m t", t=PACK))
 
-        def deal(copy, dealt, raw):
-            copy(dealt.rearrange("p (t m) -> p m t", t=PACK), raw.rearrange("p (m t) -> p m t", t=PACK))
+        def raw_sc(i):
+            return scales[:, W0 + i * R : W0 + (i + 1) * R]
 
         dealt_w = [sb.tile([P, R], U32, align_bytes=64, name="dealt_w%d" % i) for i in range(4)]
         dealt_sc = [sb.tile([P, R], U8, align_bytes=64, name="dealt_sc%d" % i) for i in range(4)]
-        deal(nc.vector.tensor_copy, dealt_w[0][:], w_raw[:])
-        tz_sb = sb.tile([P, PACK, E], F32, align_bytes=64, tag="w_then_tz")
-        tz_rows = tz.rearrange("(p t) e -> p t e", t=PACK)
-        for t in range(PACK):
-            nc.sync.dma_start(tz_sb[:, t, :], tz_rows[:, t, :])
-        deal(nc.vector.tensor_copy, dealt_w[1][:], w2_raw[:])
-        for i in range(4):
-            deal(nc.vector.tensor_copy, dealt_sc[i][:], scales[:, W0 + i * R : W0 + (i + 1) * R])
-        deal(nc.vector.tensor_copy, dealt_w[2][:], wb_raw[:])
-        deal(nc.vector.tensor_copy, dealt_w[3][:], late_w[:, 0:N])
+        deal(dealt_w[0][:], w_raw[:])
+        deal(dealt_w[1][:], w2_raw[:])
+        deal(dealt_sc[0][:], raw_sc(0))
+        deal(dealt_sc[1][:], raw_sc(1))
+        deal(dealt_w[2][:], wb_raw[:])
+        deal(dealt_sc[2][:], raw_sc(2))
+        deal(dealt_sc[3][:], raw_sc(3))
+        deal(dealt_w[3][:], late_w[:, 0:N])
+
 
         def passes(bank, i, moving, moving_sc, start, stop):
             for t in range(PACK):
@@ -116,51 +126,56 @@ def tile_list_crossed_direct_skip_tabled_pl_kernel(
                     rhs=moving, rhs_scale=moving_sc, start=(start and t == 0), stop=(stop and t == PACK - 1),
                 )
 
-        hid_w = sb.tile([P, J], U32, align_bytes=64)
+        halves = [slice(h * HALF, (h + 1) * HALF) for h in range(2)]
+        a = [psum.tile([P, PACK, HALF], F32, name="a%d" % h) for h in range(2)]
+        b = [psum.tile([P, PACK, HALF], F32, name="b%d" % h) for h in range(2)]
+        acc = [psum.tile([P, PACK, HALF], F32, name="acc%d" % h) for h in range(2)]
+        hid_w = [sb.tile([P, HALF], U32, align_bytes=64, name="hid_w%d" % h) for h in range(2)]
         hid_sc = [sb.tile([P, HALF], U8, align_bytes=64, name="hid_sc%d" % h) for h in range(2)]
-        for h in range(2):
-            js = slice(h * HALF, (h + 1) * HALF)
-            xt_h = xt_g[:, js].bitcast(E4M3)
-            xo_h = xo_g[:, js].bitcast(E2M1)
-            xt_s = scales[:, XT0 + h * HALF : XT0 + (h + 1) * HALF]
-            xo_s = scales[:, XO0 + h * HALF : XO0 + (h + 1) * HALF]
-            a = psum.tile([P, PACK, HALF], F32, name="a%d" % h)
-            b = psum.tile([P, PACK, HALF], F32, name="b%d" % h)
-            passes(a, 0, xt_h, xt_s, True, False)
-            passes(a, 1, xo_h, xo_s, False, True)
-            passes(b, 1, xt_h, xt_s, True, False)
-            passes(b, 0, xo_h, xo_s, False, True)
+        for h, js in enumerate(halves):
+            xt_h = (xt_g[:, js].bitcast(E4M3), scales[:, XT0 + h * HALF : XT0 + (h + 1) * HALF])
+            xo_h = (xo_g[:, js].bitcast(E2M1), scales[:, XO0 + h * HALF : XO0 + (h + 1) * HALF])
+            passes(a[h], 0, *xt_h, True, False)
+            passes(a[h], 1, *xo_h, False, True)
+            passes(b[h], 1, *xt_h, True, False)
+            passes(b[h], 0, *xo_h, False, True)
             a_sb = sb.tile([P, HALF, PACK], F32, name="a_sb%d" % h)
-            nc.scalar.activation(a_sb[:], a[:].rearrange("p t j -> p j t"), ACT.Copy)
+            nc.scalar.activation(a_sb[:], a[h][:].rearrange("p t j -> p j t"), ACT.Copy)
             hid = sb.tile([P, HALF, PACK], BF16, align_bytes=64, name="hid%d" % h)
-            nc.vector.tensor_tensor(hid[:], b[:].rearrange("p t j -> p j t"), a_sb[:], ALU.max)
-            nc.vector.quantize_mx(hid_w[:, js].bitcast(E4M3), hid_sc[h][:], hid[:].rearrange("p j t -> p (j t)"))
+            nc.vector.tensor_tensor(hid[:], b[h][:].rearrange("p t j -> p j t"), a_sb[:], ALU.max)
+            nc.vector.quantize_mx(hid_w[h][:].bitcast(E4M3), hid_sc[h][:], hid[:].rearrange("p j t -> p (j t)"))
+        sx_w = late_w[:, N:].bitcast(U16)
+        for h, js in enumerate(halves):
+            passes(acc[h], 3, sx_w[:, js].bitcast(E2M1), scales[:, SX0 + h * HALF : SX0 + (h + 1) * HALF], True, False)
+            passes(acc[h], 2, hid_w[h][:].bitcast(E4M3), hid_sc[h][:], False, True)
 
-        tz_g = sb.tile([P, PACK, J], F32)
-        for t in range(PACK):
+        LAST = PACK - 1
+        tz_g = sb.tile([P, LAST, J], F32)
+        for t in range(LAST):
             nc.scalar.activation(tz_g[:, t, :], tz_sb[:, t, :].indirect(l_tz[:]), ACT.Copy)
+        tz_last = [sb.tile([P, HALF], F32, name="tz_last%d" % h) for h in range(2)]
+        for h in range(2):
+            nc.scalar.activation(tz_last[h][:], tz_sb[:, LAST, :].indirect(l_tz[:, 8 * h : 8 * h + 8]), ACT.Copy)
+
+        y = sb.tile([P, PACK, J], F32)
+        out_rows = out_0.rearrange("(p t) j -> p t j", t=PACK)
+        for h, js in enumerate(halves):
+            nc.vector.tensor_tensor(y[:, 0:LAST, js], acc[h][:, 0:LAST, :], tz_g[:, :, js], ALU.add)
+        nc.sync.dma_start(out_rows[:, 0:LAST, :], y[:, 0:LAST, :])
+        for h, js in enumerate(halves):
+            nc.vector.tensor_tensor(y[:, LAST, js], acc[h][:, LAST, :], tz_last[h][:], ALU.add)
+        nc.sync.dma_start(out_rows[:, LAST, :], y[:, LAST, :])
 
         y_w = sb.tile([P, J], U32, align_bytes=64)
         y_sc = sb.tile([P, J], U8, align_bytes=64)
-        out_rows = out_0.rearrange("(p t) j -> p t j", t=PACK)
         out_words = words8(out_1)
-        sx_w = late_w[:, N:].bitcast(U16)
-        for h in range(2):
-            js = slice(h * HALF, (h + 1) * HALF)
-            acc = psum.tile([P, PACK, HALF], F32, name="acc%d" % h)
-            passes(acc, 3, sx_w[:, js].bitcast(E2M1), scales[:, SX0 + h * HALF : SX0 + (h + 1) * HALF], True, False)
-            passes(acc, 2, hid_w[:, js].bitcast(E4M3), hid_sc[h][:], False, True)
-            y = sb.tile([P, PACK, HALF], F32, name="y%d" % h)
-            nc.vector.tensor_tensor(y[:], acc[:], tz_g[:, :, js], ALU.add)
-            nc.sync.dma_start(out_rows[:, :, js], y[:])
-            y_bf = sb.tile([P, HALF, PACK], BF16, align_bytes=64, name="y_bf%d" % h)
-            if h == 0:
-                nc.scalar.copy(y_bf[:], y[:].rearrange("p t j -> p j t"))
-            else:
-                nc.vector.tensor_copy(y_bf[:], y[:].rearrange("p t j -> p j t"))
-            nc.vector.quantize_mx(y_w[:, js].bitcast(E4M3), y_sc[:, js], y_bf[:].rearrange("p j t -> p (j t)"))
+        y_bf = [sb.tile([P, HALF, PACK], BF16, align_bytes=64, name="y_bf%d" % h) for h in range(2)]
+        nc.scalar.copy(y_bf[0][:], y[:, :, halves[0]].rearrange("p t j -> p j t"))
+        nc.vector.tensor_copy(y_bf[1][:], y[:, :, halves[1]].rearrange("p t j -> p j t"))
+        for h, js in enumerate(halves):
+            nc.vector.quantize_mx(y_w[:, js].bitcast(E4M3), y_sc[:, js], y_bf[h][:].rearrange("p j t -> p (j t)"))
             nc.sync.dma_start(out_words[:, js], y_w[:, js].bitcast(I32))
         out_sc = out_2[0].bitcast(I32)
         for q in range(4):
-            eng = nc.scalar if q % 2 else nc.sync
+            eng = nc.sync if q % 2 else nc.scalar
             eng.dma_start(out_sc[4 * q : 4 * q + 4, :], y_sc[32 * q : 32 * q + 4, :].bitcast(I32))

from contextlib import ExitStack

import concourse.mybir as mybir

K, T, Z, J, R, N, L, E = 512, 1024, 1024, 256, 512, 512, 512, 1024
FLOPS = 2 * 512 * 512 * 256 * 6

F32 = mybir.dt.float32
BF16 = mybir.dt.bfloat16
I32 = mybir.dt.int32
U32 = mybir.dt.uint32
U16 = mybir.dt.uint16
U8 = mybir.dt.uint8
E4M3 = mybir.dt.float8_e4m3fn_x4
E5M2 = mybir.dt.float8_e5m2_x4
E2M1 = mybir.dt.float4_e2m1fn_x4
ACT = mybir.ActivationFunctionType
ALU = mybir.AluOpType

P = 128
PACK = 4
HALF = J // 2
ROWS = 16

XT0, XO0, W0 = 0, J, 2 * J
SX0 = W0 + 4 * R
SCALE_COLS = SX0 + J


def words8(ap):
    return ap[0].rearrange("p c r -> p (c r)").bitcast(I32)


def tile_list_crossed_direct_skip_tabled_pl_kernel(
    tc, xt_words, xt_scales, xo_words, xo_scales, w_words, w_scales, w2_words, w2_scales,
    wb_words, wb_scales, sx_words, sx_scales, ws_words, ws_scales, tz, offs, offs2, offs3,
    out_0, out_1, out_2,
):
    nc = tc.nc
    with ExitStack() as ctx:
        lists = ctx.enter_context(tc.tile_pool(name="lists", bufs=1))
        sb = ctx.enter_context(tc.tile_pool(name="sb", bufs=1))
        shared = ctx.enter_context(tc.tile_pool(name="shared", bufs=1))
        psum = ctx.enter_context(tc.psum_pool(name="psum", bufs=1))

        l_xt = lists.tile([P, J // 16], U16)
        l_xo = lists.tile([P, J // 16], U16)
        l_tz = lists.tile([P, J // 16], U16)

        xt_sc = sb.tile([P, T], U8, align_bytes=64)
        xo_sc = sb.tile([P, Z], U8, align_bytes=64)
        scales = sb.tile([P, SCALE_COLS], U8, align_bytes=64)
        staged = sb.tile([ROWS, SCALE_COLS], U8, align_bytes=64)
        sx_sc = shared.tile([ROWS, J], U8, align_bytes=64, offset=2432)
        nc.vector.memset(xt_sc[:].bitcast(I32), 0)
        nc.vector.memset(xo_sc[:].bitcast(I32), 0)
        nc.vector.memset(scales[:].bitcast(I32), 0)

        xt_w = sb.tile([P, T], U32, align_bytes=64)
        xo_w = sb.tile([P, Z], U16, align_bytes=64)
        w_raw = sb.tile([P, R], U32, align_bytes=64)
        w2_raw = sb.tile([P, R], U32, align_bytes=64)
        wb_raw = sb.tile([P, N], U32, align_bytes=64)

        small = nc.sync
        nc.sync.dma_start(l_xt[:], offs)
        nc.sync.dma_start(l_xo[:], offs2)
        small.dma_start(xt_sc[0:ROWS, :].bitcast(I32), xt_scales[0].bitcast(I32))
        small.dma_start(xo_sc[0:ROWS, :].bitcast(I32), xo_scales[0].bitcast(I32))
        nc.sync.dma_start(xt_w[:].bitcast(I32), words8(xt_words))
        nc.sync.dma_start(xo_w[:].bitcast(I32), xo_words[0].bitcast(I32))
        for i, sc in enumerate((w_scales, w2_scales, wb_scales, ws_scales)):
            small.dma_start(staged[:, W0 + i * R : W0 + (i + 1) * R].bitcast(I32), sc[0].bitcast(I32))
        small.dma_start(sx_sc[:].bitcast(I32), sx_scales[0].bitcast(I32))
        nc.sync.dma_start(w_raw[:].bitcast(I32), words8(w_words))
        nc.sync.dma_start(w2_raw[:].bitcast(I32), words8(w2_words))
        nc.sync.dma_start(l_tz[:], offs3)
        nc.sync.dma_start(wb_raw[:].bitcast(I32), words8(wb_words))

        xt_sc_g = sb.tile([P, J], U8, align_bytes=64)
        xo_sc_g = sb.tile([P, J], U8, align_bytes=64)
        nc.vector.tensor_copy(xt_sc_g[:], xt_sc[:].indirect(l_xt[:]))
        nc.vector.tensor_copy(xo_sc_g[:], xo_sc[:].indirect(l_xo[:]))
        nc.vector.tensor_copy(staged[:, XT0 : XT0 + J].bitcast(I32), xt_sc_g[0:ROWS, :].bitcast(I32))
        nc.vector.tensor_copy(staged[:, XO0 : XO0 + J].bitcast(I32), xo_sc_g[0:ROWS, :].bitcast(I32))
        nc.scalar.copy(staged[:, SX0:].bitcast(U32), sx_sc[:].bitcast(U32))
        for q in range(4):
            nc.sync.dma_start(scales[32 * q : 32 * q + 4, :].bitcast(I32), staged[4 * q : 4 * q + 4, :].bitcast(I32))

        late_w = shared.tile([P, N + J // 2], U32, align_bytes=64, offset=0)
        tz_sb = shared.tile([P, PACK, E], F32, align_bytes=64, offset=2560)
        nc.sync.dma_start(late_w[:, 0:N].bitcast(I32), words8(ws_words))
        nc.sync.dma_start(late_w[:, N:].bitcast(I32), sx_words[0].bitcast(I32))
        tz_rows = tz.rearrange("(p t) e -> p t e", t=PACK)
        for t in range(PACK):
            nc.sync.dma_start(tz_sb[:, t, :], tz_rows[:, t, :])

        xt_g = sb.tile([P, J], U32, align_bytes=64)
        xo_g = sb.tile([P, J], U16, align_bytes=64)
        nc.vector.tensor_copy(xt_g[:], xt_w[:].indirect(l_xt[:]))
        nc.vector.tensor_copy(xo_g[:], xo_w[:].indirect(l_xo[:]))

        def deal(dealt, raw):
            nc.vector.tensor_copy(dealt.rearrange("p (t m) -> p m t", t=PACK), raw.rearrange("p (m t) -> p m t", t=PACK))

        def raw_sc(i):
            return scales[:, W0 + i * R : W0 + (i + 1) * R]

        dealt_w = [sb.tile([P, R], U32, align_bytes=64, name="dealt_w%d" % i) for i in range(4)]
        dealt_sc = [sb.tile([P, R], U8, align_bytes=64, name="dealt_sc%d" % i) for i in range(4)]
        deal(dealt_w[0][:], w_raw[:])
        deal(dealt_w[1][:], w2_raw[:])
        deal(dealt_sc[0][:], raw_sc(0))
        deal(dealt_sc[1][:], raw_sc(1))
        deal(dealt_w[2][:], wb_raw[:])
        deal(dealt_sc[2][:], raw_sc(2))
        deal(dealt_sc[3][:], raw_sc(3))
        deal(dealt_w[3][:], late_w[:, 0:N])


        def passes(bank, i, moving, moving_sc, start, stop):
            for t in range(PACK):
                cols = slice(t * P, (t + 1) * P)
                nc.tensor.matmul_mx(
                    bank[:, t, :], lhsT=dealt_w[i][:, cols].bitcast(E5M2), lhsT_scale=dealt_sc[i][:, cols],
                    rhs=moving, rhs_scale=moving_sc, start=(start and t == 0), stop=(stop and t == PACK - 1),
                )

        halves = [slice(h * HALF, (h + 1) * HALF) for h in range(2)]
        a = [psum.tile([P, PACK, HALF], F32, name="a%d" % h) for h in range(2)]
        b = [psum.tile([P, PACK, HALF], F32, name="b%d" % h) for h in range(2)]
        acc = [psum.tile([P, PACK, HALF], F32, name="acc%d" % h) for h in range(2)]
        hid_w = [sb.tile([P, HALF], U32, align_bytes=64, name="hid_w%d" % h) for h in range(2)]
        hid_sc = [sb.tile([P, HALF], U8, align_bytes=64, name="hid_sc%d" % h) for h in range(2)]
        for h, js in enumerate(halves):
            xt_h = (xt_g[:, js].bitcast(E4M3), scales[:, XT0 + h * HALF : XT0 + (h + 1) * HALF])
            xo_h = (xo_g[:, js].bitcast(E2M1), scales[:, XO0 + h * HALF : XO0 + (h + 1) * HALF])
            passes(a[h], 0, *xt_h, True, False)
            passes(a[h], 1, *xo_h, False, True)
            passes(b[h], 1, *xt_h, True, False)
            passes(b[h], 0, *xo_h, False, True)
            a_sb = sb.tile([P, HALF, PACK], F32, name="a_sb%d" % h)
            nc.scalar.activation(a_sb[:], a[h][:].rearrange("p t j -> p j t"), ACT.Copy)
            hid = sb.tile([P, HALF, PACK], BF16, align_bytes=64, name="hid%d" % h)
            nc.vector.tensor_tensor(hid[:], b[h][:].rearrange("p t j -> p j t"), a_sb[:], ALU.max)
            nc.vector.quantize_mx(hid_w[h][:].bitcast(E4M3), hid_sc[h][:], hid[:].rearrange("p j t -> p (j t)"))
        sx_w = late_w[:, N:].bitcast(U16)
        for h, js in enumerate(halves):
            passes(acc[h], 3, sx_w[:, js].bitcast(E2M1), scales[:, SX0 + h * HALF : SX0 + (h + 1) * HALF], True, False)
            passes(acc[h], 2, hid_w[h][:].bitcast(E4M3), hid_sc[h][:], False, True)

        LAST = PACK - 1
        tz_g = sb.tile([P, LAST, J], F32)
        for t in range(LAST):
            nc.scalar.activation(tz_g[:, t, :], tz_sb[:, t, :].indirect(l_tz[:]), ACT.Copy)
        tz_last = [sb.tile([P, HALF], F32, name="tz_last%d" % h) for h in range(2)]
        for h in range(2):
            nc.scalar.activation(tz_last[h][:], tz_sb[:, LAST, :].indirect(l_tz[:, 8 * h : 8 * h + 8]), ACT.Copy)

        y = sb.tile([P, PACK, J], F32)
        out_rows = out_0.rearrange("(p t) j -> p t j", t=PACK)
        for h, js in enumerate(halves):
            nc.vector.tensor_tensor(y[:, 0:LAST, js], acc[h][:, 0:LAST, :], tz_g[:, :, js], ALU.add)
        nc.sync.dma_start(out_rows[:, 0:LAST, :], y[:, 0:LAST, :])
        for h, js in enumerate(halves):
            nc.vector.tensor_tensor(y[:, LAST, js], acc[h][:, LAST, :], tz_last[h][:], ALU.add)
        nc.sync.dma_start(out_rows[:, LAST, :], y[:, LAST, :])

        y_w = sb.tile([P, J], U32, align_bytes=64)
        y_sc = sb.tile([P, J], U8, align_bytes=64)
        out_words = words8(out_1)
        y_bf = [sb.tile([P, HALF, PACK], BF16, align_bytes=64, name="y_bf%d" % h) for h in range(2)]
        nc.scalar.copy(y_bf[0][:], y[:, :, halves[0]].rearrange("p t j -> p j t"))
        nc.vector.tensor_copy(y_bf[1][:], y[:, :, halves[1]].rearrange("p t j -> p j t"))
        for h, js in enumerate(halves):
            nc.vector.quantize_mx(y_w[:, js].bitcast(E4M3), y_sc[:, js], y_bf[h][:].rearrange("p j t -> p (j t)"))
            nc.sync.dma_start(out_words[:, js], y_w[:, js].bitcast(I32))
        out_sc = out_2[0].bitcast(I32)
        for q in range(4):
            eng = nc.sync if q % 2 else nc.scalar
            eng.dma_start(out_sc[4 * q : 4 * q + 4, :], y_sc[32 * q : 32 * q + 4, :].bitcast(I32))
